import numpy as np
import ml_dtypes


def mxq(x, axis, fmt="e4m3"):
    dtype, down = {"e4m3": (ml_dtypes.float8_e4m3fn, 7), "e5m2": (ml_dtypes.float8_e5m2, 14)}[fmt]
    v = np.moveaxis(np.asarray(x, np.float32).astype(ml_dtypes.bfloat16).astype(np.float64), axis, -1)
    blocks = v.reshape(v.shape[:-1] + (-1, 32))
    amax = np.abs(blocks).max(-1, keepdims=True)
    byte = np.maximum(np.where(amax > 0, np.frexp(amax)[1] - 1 + 127, 0) - down, 1)
    scale = np.exp2(byte - 127.0)
    codes = (blocks / scale).astype(np.float32).astype(dtype).astype(np.float64)
    return np.moveaxis((codes * scale).reshape(v.shape), -1, axis)


WIDE = False


def mx_kscale(k):
    if not WIDE:
        return np.ones(k)
    levels = np.array([10, -10, 5, -5, 0])
    if k % 512:
        return np.exp2(np.random.permutation(np.resize(levels, k // 32))).repeat(32)
    a = np.empty((k // 512, 16))
    for p in range(k // 512):
        a[p, :8] = np.random.permutation(np.resize(levels, 8))
        for g in range(8):
            far = levels[np.abs(levels - a[p, g]) >= 10]
            a[p, g + 8] = far[np.random.randint(len(far))]
    return np.exp2(a.ravel()).repeat(32)


def f64(x):
    return np.asarray(x).astype(np.float64)


def striped(idx):
    return np.tile(np.asarray(idx).reshape(-1, 16).T, (8, 1)).astype(np.uint16)


def unstriped(offs):
    return offs[:16].T.reshape(-1).astype(np.int64)


E2M1 = np.array([0.0, 0.5, 1.0, 1.5, 2.0, 3.0, 4.0, 6.0, -0.0, -0.5, -1.0, -1.5, -2.0, -3.0, -4.0, -6.0])


def pack_weight(w, fmt):
    k, n = w.shape
    w = f64(np.asarray(w, np.float32).astype(ml_dtypes.bfloat16)).reshape(k // 32, 32, n)
    amax = np.abs(w).max(1)
    if fmt == "e4m3":
        byte = np.frexp(amax)[1] - 1 + 127 - 7
    else:
        mant, ex = np.frexp(amax / 6.0)
        byte = np.where(mant > 0.5, ex, ex - 1) + 127
    byte = np.clip(np.where(amax > 0, byte, 1), 1, 254)
    scaled = (w * np.exp2(127.0 - byte)[:, None, :]).reshape(k, n).astype(np.float32)
    by_word = np.ascontiguousarray(scaled.reshape(k // 512, 128, 4, n).transpose(0, 1, 3, 2))
    if fmt == "e4m3":
        words = by_word.astype(ml_dtypes.float8_e4m3fn).view(np.uint8)
    else:
        c = by_word.astype(ml_dtypes.float4_e2m1fn).view(np.uint8) & 0xF
        words = (c[..., 0::2] | (c[..., 1::2] << 4)).reshape(k // 512, 128, 2 * n)
    return np.ascontiguousarray(words), np.ascontiguousarray(byte.astype(np.uint8).reshape(k // 512, 16, n))


def unpack_weight(words, scales, fmt):
    g, _, n = scales.shape
    words = np.ascontiguousarray(words).reshape(g, 128, n, -1)
    if fmt == "e4m3":
        vals = words.view(ml_dtypes.float8_e4m3fn).astype(np.float64)
    else:
        nib = np.empty((g, 128, n, 4), np.uint8)
        nib[..., 0::2] = words & 0xF
        nib[..., 1::2] = words >> 4
        vals = E2M1[nib]
    vals = vals * np.repeat(np.exp2(scales.astype(np.float64) - 127.0), 8, axis=1)[..., None]
    return vals.transpose(0, 1, 3, 2).reshape(g * 512, n)


def sigmoid(v):
    return 1.0 / (1.0 + np.exp(-v))


def sgn(shape):
    return np.random.uniform(0.5, 2.0, shape) * np.where(np.random.standard_normal(shape) < 0, -1.0, 1.0)


K, T, J, R, F, Z, N, C, O = 512, 1024, 256, 512, 512, 1024, 256, 512, 128


def setup_inputs():
    n = np.random.standard_normal
    idx = np.random.permutation(T)[:J]
    idx2 = np.random.permutation(Z)[:J]
    idx3 = np.random.permutation(C)[:J]
    idx4 = np.random.permutation(C)[:J]
    idx5 = np.random.permutation(J)[:O]
    idx6 = np.random.permutation(J)[:O]
    ff = mx_kscale(F)
    fk = mx_kscale(K)
    fr = mx_kscale(R)
    xop = pack_weight(n((F, Z)) / ff[:, None], "e4m3")
    wp = pack_weight(n((K, R)) * 1 / np.sqrt(K) / fk[:, None] * fr, "e2m1")
    w2p = pack_weight(n((F, R)) * 1 / np.sqrt(F) * ff[:, None] * fr, "e2m1")
    wbp = pack_weight(n((R, N)) * 1 / np.sqrt(R) / fr[:, None], "e2m1")
    wcp = pack_weight(n((R, N)) * 1 / np.sqrt(R) / fr[:, None], "e4m3")
    return {
        "xo_words": xop[0],
        "xo_scales": xop[1],
        "cq": (np.random.randint(-7, 8, (K, T)).astype(np.float64)).astype(np.float32),
        "gs": (np.random.uniform(0.1, 0.4, (K, 1)) * fk[:, None]).astype(np.float32),
        "w_words": wp[0],
        "w_scales": wp[1],
        "w2_words": w2p[0],
        "w2_scales": w2p[1],
        "wb_words": wbp[0],
        "wb_scales": wbp[1],
        "wc_words": wcp[0],
        "wc_scales": wcp[1],
        "so": (np.random.uniform(0.5, 1.6, (N, 1))).astype(np.float32),
        "sp": (sgn((N, 1))).astype(np.float32),
        "bo": (np.random.uniform(-2.0, 2.0, (N, 1))).astype(np.float32),
        "offs": striped(idx),
        "offs2": striped(idx2),
        "offs3": striped(idx3),
        "offs4": striped(idx4),
        "offs5": striped(idx5),
        "offs6": striped(idx6),
    }


def reference(xo_words, xo_scales, cq, gs, w_words, w_scales, w2_words, w2_scales, wb_words, wb_scales, wc_words, wc_scales, so, sp, bo, offs, offs2, offs3, offs4, offs5, offs6):
    idx = unstriped(offs)
    idx2 = unstriped(offs2)
    idx3 = unstriped(offs3)
    idx4 = unstriped(offs4)
    idx5 = unstriped(offs5)
    idx6 = unstriped(offs6)
    xou = unpack_weight(xo_words, xo_scales, "e4m3")
    wu = unpack_weight(w_words, w_scales, "e2m1")
    w2u = unpack_weight(w2_words, w2_scales, "e2m1")
    wbu = unpack_weight(wb_words, wb_scales, "e2m1")
    wcu = unpack_weight(wc_words, wc_scales, "e4m3")
    x1 = f64(cq)[:, idx] * f64(gs)
    x1q = mxq(x1, 0, "e4m3")
    a = wu.T @ x1q
    xoidx2g = xou[:, idx2]
    b = w2u.T @ xoidx2g
    hid = np.maximum(a, b)
    hidq = mxq(hid, 0, "e4m3")
    p = wbu.T @ hidq
    q = wcu.T @ hidq
    pw = np.zeros((N, C))
    pw[:, idx3] = p
    m0 = np.maximum(pw[:, idx4], q)
    y = m0[:, idx5] * f64(so) * sigmoid(m0[:, idx6] * f64(sp) + f64(bo))
    return y

@@ -1,0 +1,242 @@
+from contextlib import ExitStack
+
+import concourse.mybir as mybir
+
+K, T, J, R, F, Z, N, C, O = 512, 1024, 256, 512, 512, 1024, 256, 512, 128
+FLOPS = 2 * J * (K * R + F * R + 2 * R * N)
+
+F32 = mybir.dt.float32
+BF16 = mybir.dt.bfloat16
+I32 = mybir.dt.int32
+U32 = mybir.dt.uint32
+U16 = mybir.dt.uint16
+U8 = mybir.dt.uint8
+FP8X4 = mybir.dt.float8_e4m3fn_x4
+FP4X4 = mybir.dt.float4_e2m1fn_x4
+ACT = mybir.ActivationFunctionType
+ALU = mybir.AluOpType
+
+P = 128
+PACK = 4
+HALF = J // 2
+LIST_COLS = HALF // 16
+
+
+def tile_list_outcomegatedchain_codednote_kernel(
+    tc, xo_words, xo_scales, cq, gs, w_words, w_scales, w2_words, w2_scales,
+    wb_words, wb_scales, wc_words, wc_scales, so, sp, bo,
+    offs, offs2, offs3, offs4, offs5, offs6, out,
+):
+    nc = tc.nc
+    with ExitStack() as ctx:
+        sb = ctx.enter_context(tc.tile_pool(name="sb", bufs=1))
+        ps = ctx.enter_context(tc.psum_pool(name="ps", bufs=1))
+
+        def load_list(src, name):
+            dst = sb.tile(list(src.shape), U16, name=name)
+            nc.sync.dma_start(dst[:], src)
+            return dst
+
+        def stage_scales(stage, col, scales, queues):
+            width = scales.shape[2] // 4
+            rows = scales[0].bitcast(I32)
+            for pair in range(2):
+                queues[pair].dma_start(
+                    out=stage[64 * pair : 64 * pair + 4, :, col : col + width],
+                    in_=rows[8 * pair : 8 * pair + 8, :].rearrange("(q r) n -> r q n", r=4),
+                )
+
+        def spread_scales(plane, stage):
+            words = plane[:].bitcast(I32)
+            for q in range(4):
+                src = 64 * (q // 2)
+                nc.vector.tensor_copy(out=words[32 * q : 32 * q + 4, :], in_=stage[src : src + 4, q % 2, :])
+
+        cq_rows = cq.rearrange("(p t) n -> t p n", t=PACK)
+        cq_sb = [sb.tile([P, T], F32, name=f"cq{t}") for t in range(PACK)]
+
+        gs_sb = sb.tile([P, PACK], F32)
+        nc.gpsimd.dma_start(out=gs_sb[:], in_=gs.rearrange("(p t) o -> p (t o)", t=PACK))
+
+        l1 = load_list(offs, "l1")
+        ww_stage = sb.tile([P, 2, 2 * R // 4], I32)
+        stage_scales(ww_stage, 0, w_scales, (nc.scalar, nc.sync))
+        nc.scalar.dma_start(out=cq_sb[0][:], in_=cq_rows[0])
+        stage_scales(ww_stage, R // 4, w2_scales, (nc.sync, nc.sync))
+        l2 = load_list(offs2, "l2")
+        w_raw = sb.tile([P, R], U16)
+        w2_raw = sb.tile([P, R], U16)
+        xo_stage = sb.tile([P, 2, Z // 4], I32)
+        xo_sb = sb.tile([P, Z], I32)
+        nc.sync.dma_start(out=cq_sb[1][:], in_=cq_rows[1])
+        nc.sync.dma_start(out=cq_sb[2][:], in_=cq_rows[2])
+        stage_scales(xo_stage, 0, xo_scales, (nc.sync, nc.sync))
+        nc.sync.dma_start(out=cq_sb[3][:], in_=cq_rows[3])
+        nc.sync.dma_start(out=w_raw[:].bitcast(I32), in_=w_words[0].bitcast(I32))
+        nc.sync.dma_start(out=w2_raw[:].bitcast(I32), in_=w2_words[0].bitcast(I32))
+        nc.sync.dma_start(out=xo_sb[:], in_=xo_words[0].rearrange("p n t -> p (n t)").bitcast(I32))
+        bc_stage = sb.tile([4, 4, 2 * N // 4], I32)
+        for col, scales in ((0, wb_scales), (N // 4, wc_scales)):
+            nc.sync.dma_start(
+                out=bc_stage[:, :, col : col + N // 4],
+                in_=scales[0].bitcast(I32).rearrange("(q r) n -> r q n", r=4),
+            )
+        wb_sb = sb.tile([P, N], U16, align_bytes=64)
+        nc.sync.dma_start(out=wb_sb[:].bitcast(I32), in_=wb_words[0].bitcast(I32))
+        l3 = load_list(offs3, "l3")
+        wc_sb = sb.tile([P, N], I32, align_bytes=64)
+        nc.sync.dma_start(out=wc_sb[:], in_=wc_words[0].rearrange("p n t -> p (n t)").bitcast(I32))
+        l4 = load_list(offs4, "l4")
+        l6 = load_list(offs6, "l6")
+        l5 = load_list(offs5, "l5")
+        per_row = []
+        with nc.allow_non_contiguous_dma(reason="one value a partition for each block of 128 output features"):
+            for name, src in (("so_sb", so), ("sp_sb", sp), ("bo_sb", bo)):
+                dst = sb.tile([P, 2], F32, name=name)
+                nc.sync.dma_start(out=dst[:], in_=src.rearrange("(h p) o -> p (h o)", p=P))
+                per_row.append(dst)
+        so_sb, sp_sb, bo_sb = per_row
+
+
+        ww_plane = sb.tile([P, 2 * R], U8)
+        xo_plane = sb.tile([P, Z], U8)
+        bc_plane = sb.tile([P, 2 * N], U8, align_bytes=64)
+        for plane in (ww_plane, xo_plane, bc_plane):
+            nc.vector.memset(plane[:].bitcast(I32), 0)
+        board = [sb.tile([P, C], F32, name=f"board{h}") for h in range(2)]
+        for h in range(2):
+            nc.vector.memset(board[h][:], 0.0)
+
+        spread_scales(ww_plane, ww_stage)
+        ww_scale = sb.tile([P, 2 * R], U8, align_bytes=64)
+        nc.vector.tensor_copy(
+            out=ww_scale[:].rearrange("p (w t m) -> p w t m", w=2, t=PACK),
+            in_=ww_plane[:].rearrange("p (w m t) -> p w t m", w=2, t=PACK),
+        )
+        w_sb = sb.tile([P, R], U16, align_bytes=64)
+        w2_sb = sb.tile([P, R], U16, align_bytes=64)
+
+        x1 = sb.tile([P, PACK, J], BF16)
+        for t in range(PACK):
+            nc.scalar.activation(
+                out=x1[:, t, :], in_=cq_sb[t][:].indirect(l1[:]), func=ACT.Copy, scale=gs_sb[:, t : t + 1]
+            )
+
+        spread_scales(xo_plane, xo_stage)
+        xo_scale = sb.tile([P, J], U8, align_bytes=64)
+        nc.vector.tensor_copy(out=xo_scale[:], in_=xo_plane[:].indirect(l2[:]))
+
+        def half_cols(u):
+            return slice(u * HALF, (u + 1) * HALF)
+
+        def half_list(lst, u):
+            return lst[:, u * LIST_COLS : (u + 1) * LIST_COLS]
+
+        def block(t):
+            return slice(t * P, (t + 1) * P)
+
+        def quantise(values, name):
+            codes = sb.tile([P, HALF], U32, name=name + "_codes", align_bytes=64)
+            scale = sb.tile([P, HALF], U8, name=name + "_scale", align_bytes=64)
+            nc.vector.quantize_mx(
+                out=codes[:].bitcast(FP8X4), scales=scale[:], in_=values[:].rearrange("p j t -> p (j t)")
+            )
+            return codes, scale
+
+        nc.vector.tensor_copy(
+            out=w_sb[:].rearrange("p (t m) -> p t m", t=PACK), in_=w_raw[:].rearrange("p (m t) -> p t m", t=PACK)
+        )
+        x1_woven = [sb.tile([P, HALF, PACK], BF16, name=f"x1w{u}", align_bytes=64) for u in range(2)]
+        for u, weave in enumerate((nc.vector.tensor_copy, nc.scalar.copy)):
+            weave(
+                out=x1_woven[u][:].rearrange("p (c i) t -> p c t i", i=4),
+                in_=x1[:, :, half_cols(u)].rearrange("p t (c i) -> p c t i", i=4),
+            )
+        nc.scalar.copy(
+            out=w2_sb[:].rearrange("p (t m) -> p t m", t=PACK), in_=w2_raw[:].rearrange("p (m t) -> p t m", t=PACK)
+        )
+        a_sb = []
+        b_ps = []
+        for u in range(2):
+            codes, scale = quantise(x1_woven[u], f"x1q{u}")
+            dst = sb.tile([P, 2, HALF, 2], F32, name=f"a_sb{u}")
+            for pair in range(2):
+                a_ps = ps.tile([P, 2, HALF], F32, name=f"a_ps{u}{pair}", tag=f"bank{u}{pair}")
+                for e in range(2):
+                    t = 2 * pair + e
+                    nc.tensor.matmul_mx(
+                        out=a_ps[:, e, :], lhsT=w_sb[:, block(t)].bitcast(FP4X4), lhsT_scale=ww_scale[:, block(t)],
+                        rhs=codes[:].bitcast(FP8X4), rhs_scale=scale[:], start=True, stop=True,
+                    )
+                nc.scalar.copy(out=dst[:, pair, :, :], in_=a_ps[:].rearrange("p e j -> p j e"))
+            a_sb.append(dst)
+
+            picked = sb.tile([P, HALF], U32, name=f"xo_pick{u}", align_bytes=64)
+            nc.vector.tensor_copy(out=picked[:], in_=xo_sb[:].bitcast(U32).indirect(half_list(l2, u)))
+            bank = ps.tile([P, PACK, HALF], F32, name=f"b_ps{u}")
+            for t in range(PACK):
+                nc.tensor.matmul_mx(
+                    out=bank[:, t, :], lhsT=w2_sb[:, block(t)].bitcast(FP4X4),
+                    lhsT_scale=ww_scale[:, block(PACK + t)],
+                    rhs=picked[:].bitcast(FP8X4), rhs_scale=xo_scale[:, half_cols(u)], start=True, stop=True,
+                )
+            b_ps.append(bank)
+
+        for q in range(4):
+            nc.vector.tensor_copy(out=bc_plane[:].bitcast(I32)[32 * q : 32 * q + 4, :], in_=bc_stage[:, q, :])
+
+        p_ps = [[ps.tile([P, HALF], F32, name=f"p_ps{h}{u}", tag=f"bank{u}{h}") for u in range(2)] for h in range(2)]
+        q_ps = ps.tile([P, 2, J], F32, name="q_ps")
+        hidq = []
+        for u in range(2):
+            hid = sb.tile([P, HALF, PACK], BF16, name=f"hid{u}", align_bytes=64)
+            nc.vector.tensor_tensor(
+                out=hid[:].rearrange("p j (r e) -> p j r e", e=2),
+                in0=b_ps[u][:].rearrange("p (r e) j -> p j r e", e=2),
+                in1=a_sb[u][:].rearrange("p r j e -> p j r e"),
+                op=ALU.max,
+            )
+            codes, scale = quantise(hid, f"hidq{u}")
+            hidq.append((codes, scale))
+            for h in range(2):
+                nc.tensor.matmul_mx(
+                    out=p_ps[h][u][:], lhsT=wb_sb[:, block(h)].bitcast(FP4X4),
+                    lhsT_scale=bc_plane[:, block(h)],
+                    rhs=codes[:].bitcast(FP8X4), rhs_scale=scale[:], start=True, stop=True,
+                )
+        for u in range(2):
+            p_sb = [sb.tile([P, HALF], F32, name=f"p_sb{h}{u}") for h in range(2)]
+            nc.scalar.copy(out=p_sb[0][:], in_=p_ps[0][u][:])
+            if u == 0:
+                nc.scalar.copy(out=p_sb[1][:], in_=p_ps[1][u][:])
+            else:
+                nc.vector.tensor_copy(out=p_sb[1][:], in_=p_ps[1][u][:])
+            nc.scalar.activation(out=board[0][:].indirect(half_list(l3, u)), in_=p_sb[0][:], func=ACT.Copy)
+            nc.vector.tensor_copy(out=board[1][:].indirect(half_list(l3, u)), in_=p_sb[1][:])
+        for u in range(2):
+            codes, scale = hidq[u]
+            for h in range(2):
+                nc.tensor.matmul_mx(
+                    out=q_ps[:, h, half_cols(u)], lhsT=wc_sb[:, block(h)].bitcast(FP8X4),
+                    lhsT_scale=bc_plane[:, block(2 + h)],
+                    rhs=codes[:].bitcast(FP8X4), rhs_scale=scale[:], start=True, stop=True,
+                )
+
+        for h in range(2):
+            looked = sb.tile([P, J], F32, name=f"looked{h}")
+            nc.vector.tensor_copy(out=looked[:, half_cols(0)], in_=board[h][:].indirect(half_list(l4, 0)))
+            nc.scalar.activation(
+                out=looked[:, half_cols(1)], in_=board[h][:].indirect(half_list(l4, 1)), func=ACT.Copy
+            )
+            m0 = sb.tile([P, J], F32, name=f"m0_{h}")
+            nc.vector.tensor_tensor(out=m0[:], in0=q_ps[:, h, :], in1=looked[:], op=ALU.max)
+            gate = sb.tile([P, O], F32, name=f"gate{h}")
+            nc.scalar.activation(
+                out=gate[:], in_=m0[:].indirect(l6[:]), func=ACT.Sigmoid,
+                scale=sp_sb[:, h : h + 1], bias=bo_sb[:, h : h + 1],
+            )
+            kept = sb.tile([P, O], F32, name=f"kept{h}")
+            nc.scalar.activation(out=kept[:], in_=m0[:].indirect(l5[:]), func=ACT.Copy, scale=so_sb[:, h : h + 1])
+            y = sb.tile([P, O], F32, name=f"y{h}")
+            nc.vector.tensor_tensor(out=y[:], in0=kept[:], in1=gate[:], op=ALU.mult)
+            nc.sync.dma_start(out=out[block(h), :], in_=y[:])

@@ -98,6 +98,10 @@ def tile_list_outcomegatedchain_codednote_kernel(
         so_sb, sp_sb, bo_sb = per_row
 
 
+        warm_in = sb.tile([P, 1], F32)
+        warm_out = sb.tile([P, 1], F32)
+        nc.vector.memset(warm_in[:], 0.0)
+        nc.scalar.activation(out=warm_out[:], in_=warm_in[:], func=ACT.Sigmoid)
         ww_plane = sb.tile([P, 2 * R], U8)
         xo_plane = sb.tile([P, Z], U8)
         bc_plane = sb.tile([P, 2 * N], U8, align_bytes=64)

@@ -37,20 +37,13 @@ def tile_list_outcomegatedchain_codednote_kernel(
             nc.sync.dma_start(dst[:], src)
             return dst
 
-        def stage_scales(stage, col, scales, queues):
-            width = scales.shape[2] // 4
-            rows = scales[0].bitcast(I32)
-            for pair in range(2):
-                queues[pair].dma_start(
-                    out=stage[64 * pair : 64 * pair + 4, :, col : col + width],
-                    in_=rows[8 * pair : 8 * pair + 8, :].rearrange("(q r) n -> r q n", r=4),
-                )
+        def stage_scales(queue, stage, scales):
+            queue.dma_start(out=stage, in_=scales[0].bitcast(I32).rearrange("(q r) n -> r q n", r=4))
 
-        def spread_scales(plane, stage):
+        def spread_scales(plane, stage, rows):
             words = plane[:].bitcast(I32)
             for q in range(4):
-                src = 64 * (q // 2)
-                nc.vector.tensor_copy(out=words[32 * q : 32 * q + 4, :], in_=stage[src : src + 4, q % 2, :])
+                nc.vector.tensor_copy(out=words[32 * q : 32 * q + rows, :], in_=stage[:, q, :])
 
         cq_rows = cq.rearrange("(p t) n -> t p n", t=PACK)
         cq_sb = [sb.tile([P, T], F32, name=f"cq{t}") for t in range(PACK)]
@@ -58,29 +51,26 @@ def tile_list_outcomegatedchain_codednote_kernel(
         gs_sb = sb.tile([P, PACK], F32)
         nc.gpsimd.dma_start(out=gs_sb[:], in_=gs.rearrange("(p t) o -> p (t o)", t=PACK))
 
+        xo_stage = sb.tile([P, 4, Z // 4], I32)
+        nc.vector.memset(xo_stage[64:96, :, :], 0)
         l1 = load_list(offs, "l1")
-        ww_stage = sb.tile([P, 2, 2 * R // 4], I32)
-        stage_scales(ww_stage, 0, w_scales, (nc.scalar, nc.sync))
+        ww_stage = sb.tile([4, 4, 2 * R // 4], I32)
+        stage_scales(nc.scalar, ww_stage[:, :, 0 : R // 4], w_scales)
         nc.scalar.dma_start(out=cq_sb[0][:], in_=cq_rows[0])
-        stage_scales(ww_stage, R // 4, w2_scales, (nc.sync, nc.sync))
+        stage_scales(nc.sync, ww_stage[:, :, R // 4 :], w2_scales)
+        stage_scales(nc.sync, xo_stage[64:68, :, :], xo_scales)
         l2 = load_list(offs2, "l2")
         w_raw = sb.tile([P, R], U16)
         w2_raw = sb.tile([P, R], U16)
-        xo_stage = sb.tile([P, 2, Z // 4], I32)
         xo_sb = sb.tile([P, Z], I32)
-        nc.sync.dma_start(out=cq_sb[1][:], in_=cq_rows[1])
-        nc.sync.dma_start(out=cq_sb[2][:], in_=cq_rows[2])
-        stage_scales(xo_stage, 0, xo_scales, (nc.sync, nc.sync))
-        nc.sync.dma_start(out=cq_sb[3][:], in_=cq_rows[3])
+        for t in range(1, PACK):
+            nc.sync.dma_start(out=cq_sb[t][:], in_=cq_rows[t])
         nc.sync.dma_start(out=w_raw[:].bitcast(I32), in_=w_words[0].bitcast(I32))
         nc.sync.dma_start(out=w2_raw[:].bitcast(I32), in_=w2_words[0].bitcast(I32))
         nc.sync.dma_start(out=xo_sb[:], in_=xo_words[0].rearrange("p n t -> p (n t)").bitcast(I32))
         bc_stage = sb.tile([4, 4, 2 * N // 4], I32)
-        for col, scales in ((0, wb_scales), (N // 4, wc_scales)):
-            nc.sync.dma_start(
-                out=bc_stage[:, :, col : col + N // 4],
-                in_=scales[0].bitcast(I32).rearrange("(q r) n -> r q n", r=4),
-            )
+        stage_scales(nc.sync, bc_stage[:, :, 0 : N // 4], wb_scales)
+        stage_scales(nc.sync, bc_stage[:, :, N // 4 :], wc_scales)
         wb_sb = sb.tile([P, N], U16, align_bytes=64)
         nc.sync.dma_start(out=wb_sb[:].bitcast(I32), in_=wb_words[0].bitcast(I32))
         l3 = load_list(offs3, "l3")
@@ -105,13 +95,13 @@ def tile_list_outcomegatedchain_codednote_kernel(
         ww_plane = sb.tile([P, 2 * R], U8)
         xo_plane = sb.tile([P, Z], U8)
         bc_plane = sb.tile([P, 2 * N], U8, align_bytes=64)
-        for plane in (ww_plane, xo_plane, bc_plane):
+        for plane in (ww_plane, bc_plane):
             nc.vector.memset(plane[:].bitcast(I32), 0)
         board = [sb.tile([P, C], F32, name=f"board{h}") for h in range(2)]
         for h in range(2):
             nc.vector.memset(board[h][:], 0.0)
 
-        spread_scales(ww_plane, ww_stage)
+        spread_scales(ww_plane, ww_stage, 4)
         ww_scale = sb.tile([P, 2 * R], U8, align_bytes=64)
         nc.vector.tensor_copy(
             out=ww_scale[:].rearrange("p (w t m) -> p w t m", w=2, t=PACK),
@@ -120,13 +110,14 @@ def tile_list_outcomegatedchain_codednote_kernel(
         w_sb = sb.tile([P, R], U16, align_bytes=64)
         w2_sb = sb.tile([P, R], U16, align_bytes=64)
 
-        x1 = sb.tile([P, PACK, J], BF16)
+        x1_flat = sb.tile([P, PACK * J], BF16)
+        x1 = x1_flat[:].rearrange("p (t j) -> p t j", t=PACK)
         for t in range(PACK):
             nc.scalar.activation(
                 out=x1[:, t, :], in_=cq_sb[t][:].indirect(l1[:]), func=ACT.Copy, scale=gs_sb[:, t : t + 1]
             )
 
-        spread_scales(xo_plane, xo_stage)
+        spread_scales(xo_plane, xo_stage[64:96, :, :], 32)
         xo_scale = sb.tile([P, J], U8, align_bytes=64)
         nc.vector.tensor_copy(out=xo_scale[:], in_=xo_plane[:].indirect(l2[:]))
 
@@ -147,15 +138,19 @@ def tile_list_outcomegatedchain_codednote_kernel(
             )
             return codes, scale
 
+        x1_woven = [sb.tile([P, HALF, PACK], BF16, name=f"x1w{u}", align_bytes=64) for u in range(2)]
+        nc.vector.tensor_copy(
+            out=x1_woven[0][:, :, 0 : PACK - 1].rearrange("p (c i) t -> p c t i", i=4),
+            in_=x1[:, 0 : PACK - 1, half_cols(0)].rearrange("p t (c i) -> p c t i", i=4),
+        )
         nc.vector.tensor_copy(
             out=w_sb[:].rearrange("p (t m) -> p t m", t=PACK), in_=w_raw[:].rearrange("p (m t) -> p t m", t=PACK)
         )
-        x1_woven = [sb.tile([P, HALF, PACK], BF16, name=f"x1w{u}", align_bytes=64) for u in range(2)]
-        for u, weave in enumerate((nc.vector.tensor_copy, nc.scalar.copy)):
-            weave(
-                out=x1_woven[u][:].rearrange("p (c i) t -> p c t i", i=4),
-                in_=x1[:, :, half_cols(u)].rearrange("p t (c i) -> p c t i", i=4),
-            )
+        nc.vector.tensor_copy(out=x1_woven[0][:, :, PACK - 1], in_=x1[:, PACK - 1, half_cols(0)])
+        nc.scalar.copy(
+            out=x1_woven[1][:].rearrange("p (c i) t -> p c t i", i=4),
+            in_=x1[:, :, half_cols(1)].rearrange("p t (c i) -> p c t i", i=4),
+        )
         nc.scalar.copy(
             out=w2_sb[:].rearrange("p (t m) -> p t m", t=PACK), in_=w2_raw[:].rearrange("p (m t) -> p t m", t=PACK)
         )
@@ -186,8 +181,7 @@ def tile_list_outcomegatedchain_codednote_kernel(
                 )
             b_ps.append(bank)
 
-        for q in range(4):
-            nc.vector.tensor_copy(out=bc_plane[:].bitcast(I32)[32 * q : 32 * q + 4, :], in_=bc_stage[:, q, :])
+        spread_scales(bc_plane, bc_stage, 4)
 
         p_ps = [[ps.tile([P, HALF], F32, name=f"p_ps{h}{u}", tag=f"bank{u}{h}") for u in range(2)] for h in range(2)]
         q_ps = ps.tile([P, 2, J], F32, name="q_ps")
@@ -211,10 +205,7 @@ def tile_list_outcomegatedchain_codednote_kernel(
         for u in range(2):
             p_sb = [sb.tile([P, HALF], F32, name=f"p_sb{h}{u}") for h in range(2)]
             nc.scalar.copy(out=p_sb[0][:], in_=p_ps[0][u][:])
-            if u == 0:
-                nc.scalar.copy(out=p_sb[1][:], in_=p_ps[1][u][:])
-            else:
-                nc.vector.tensor_copy(out=p_sb[1][:], in_=p_ps[1][u][:])
+            nc.vector.tensor_copy(out=p_sb[1][:], in_=p_ps[1][u][:])
             nc.scalar.activation(out=board[0][:].indirect(half_list(l3, u)), in_=p_sb[0][:], func=ACT.Copy)
             nc.vector.tensor_copy(out=board[1][:].indirect(half_list(l3, u)), in_=p_sb[1][:])
         for u in range(2):

@@ -48,8 +48,6 @@ def tile_list_outcomegatedchain_codednote_kernel(
         cq_rows = cq.rearrange("(p t) n -> t p n", t=PACK)
         cq_sb = [sb.tile([P, T], F32, name=f"cq{t}") for t in range(PACK)]
 
-        gs_sb = sb.tile([P, PACK], F32)
-        nc.gpsimd.dma_start(out=gs_sb[:], in_=gs.rearrange("(p t) o -> p (t o)", t=PACK))
 
         xo_stage = sb.tile([P, 4, Z // 4], I32)
         nc.vector.memset(xo_stage[64:96, :, :], 0)
@@ -59,6 +57,8 @@ def tile_list_outcomegatedchain_codednote_kernel(
         nc.scalar.dma_start(out=cq_sb[0][:], in_=cq_rows[0])
         stage_scales(nc.sync, ww_stage[:, :, R // 4 :], w2_scales)
         stage_scales(nc.sync, xo_stage[64:68, :, :], xo_scales)
+        gs_sb = sb.tile([P, PACK], F32)
+        nc.sync.dma_start(out=gs_sb[:], in_=gs.rearrange("(p t) o -> p (t o)", t=PACK))
         l2 = load_list(offs2, "l2")
         w_raw = sb.tile([P, R], U16)
         w2_raw = sb.tile([P, R], U16)

@@ -40,26 +40,26 @@ def tile_list_outcomegatedchain_codednote_kernel(
         def stage_scales(queue, stage, scales):
             queue.dma_start(out=stage, in_=scales[0].bitcast(I32).rearrange("(q r) n -> r q n", r=4))
 
-        def spread_scales(plane, stage, rows):
+        def spread_scales(plane, stage):
             words = plane[:].bitcast(I32)
             for q in range(4):
-                nc.vector.tensor_copy(out=words[32 * q : 32 * q + rows, :], in_=stage[:, q, :])
+                nc.vector.tensor_copy(out=words[32 * q : 32 * q + 4, :], in_=stage[:, q, :])
 
         cq_rows = cq.rearrange("(p t) n -> t p n", t=PACK)
         cq_sb = [sb.tile([P, T], F32, name=f"cq{t}") for t in range(PACK)]
 
 
-        xo_stage = sb.tile([P, 4, Z // 4], I32)
-        nc.vector.memset(xo_stage[64:96, :, :], 0)
-        l1 = load_list(offs, "l1")
+        xo_rows = sb.tile([P, Z], U8)
+        nc.vector.memset(xo_rows[:].bitcast(I32), 0)
+        l2 = load_list(offs2, "l2")
         ww_stage = sb.tile([4, 4, 2 * R // 4], I32)
         stage_scales(nc.scalar, ww_stage[:, :, 0 : R // 4], w_scales)
         nc.scalar.dma_start(out=cq_sb[0][:], in_=cq_rows[0])
+        nc.sync.dma_start(out=xo_rows[:].bitcast(I32)[0:16, :], in_=xo_scales[0].bitcast(I32))
         stage_scales(nc.sync, ww_stage[:, :, R // 4 :], w2_scales)
-        stage_scales(nc.sync, xo_stage[64:68, :, :], xo_scales)
+        l1 = load_list(offs, "l1")
         gs_sb = sb.tile([P, PACK], F32)
         nc.sync.dma_start(out=gs_sb[:], in_=gs.rearrange("(p t) o -> p (t o)", t=PACK))
-        l2 = load_list(offs2, "l2")
         w_raw = sb.tile([P, R], U16)
         w2_raw = sb.tile([P, R], U16)
         xo_sb = sb.tile([P, Z], I32)
@@ -93,15 +93,24 @@ def tile_list_outcomegatedchain_codednote_kernel(
         nc.vector.memset(warm_in[:], 0.0)
         nc.scalar.activation(out=warm_out[:], in_=warm_in[:], func=ACT.Sigmoid)
         ww_plane = sb.tile([P, 2 * R], U8)
-        xo_plane = sb.tile([P, Z], U8)
+        xo_scale = sb.tile([P, J], U8, align_bytes=64)
         bc_plane = sb.tile([P, 2 * N], U8, align_bytes=64)
-        for plane in (ww_plane, bc_plane):
+        for plane in (xo_scale, ww_plane, bc_plane):
             nc.vector.memset(plane[:].bitcast(I32), 0)
         board = [sb.tile([P, C], F32, name=f"board{h}") for h in range(2)]
         for h in range(2):
             nc.vector.memset(board[h][:], 0.0)
 
-        spread_scales(ww_plane, ww_stage, 4)
+        xo_picked_rows = sb.tile([P, J], U8)
+        nc.vector.tensor_copy(out=xo_picked_rows[:], in_=xo_rows[:].indirect(l2[:]))
+        nc.vector.tensor_copy(out=xo_scale[:].bitcast(I32)[0:4, :], in_=xo_picked_rows[:].bitcast(I32)[0:4, :])
+        for q in range(1, 4):
+            nc.scalar.dma_start(
+                out=xo_scale[:].bitcast(I32)[32 * q : 32 * q + 4, :],
+                in_=xo_picked_rows[:].bitcast(I32)[4 * q : 4 * q + 4, :],
+            )
+
+        spread_scales(ww_plane, ww_stage)
         ww_scale = sb.tile([P, 2 * R], U8, align_bytes=64)
         nc.vector.tensor_copy(
             out=ww_scale[:].rearrange("p (w t m) -> p w t m", w=2, t=PACK),
@@ -117,9 +126,6 @@ def tile_list_outcomegatedchain_codednote_kernel(
                 out=x1[:, t, :], in_=cq_sb[t][:].indirect(l1[:]), func=ACT.Copy, scale=gs_sb[:, t : t + 1]
             )
 
-        spread_scales(xo_plane, xo_stage[64:96, :, :], 32)
-        xo_scale = sb.tile([P, J], U8, align_bytes=64)
-        nc.vector.tensor_copy(out=xo_scale[:], in_=xo_plane[:].indirect(l2[:]))
 
         def half_cols(u):
             return slice(u * HALF, (u + 1) * HALF)
@@ -181,7 +187,7 @@ def tile_list_outcomegatedchain_codednote_kernel(
                 )
             b_ps.append(bank)
 
-        spread_scales(bc_plane, bc_stage, 4)
+        spread_scales(bc_plane, bc_stage)
 
         p_ps = [[ps.tile([P, HALF], F32, name=f"p_ps{h}{u}", tag=f"bank{u}{h}") for u in range(2)] for h in range(2)]
         q_ps = ps.tile([P, 2, J], F32, name="q_ps")

from contextlib import ExitStack

import concourse.mybir as mybir

K, T, J, R, F, Z, N, C, O = 512, 1024, 256, 512, 512, 1024, 256, 512, 128
FLOPS = 2 * J * (K * R + F * R + 2 * R * N)

F32 = mybir.dt.float32
BF16 = mybir.dt.bfloat16
I32 = mybir.dt.int32
U32 = mybir.dt.uint32
U16 = mybir.dt.uint16
U8 = mybir.dt.uint8
FP8X4 = mybir.dt.float8_e4m3fn_x4
FP4X4 = mybir.dt.float4_e2m1fn_x4
ACT = mybir.ActivationFunctionType
ALU = mybir.AluOpType

P = 128
PACK = 4
HALF = J // 2
LIST_COLS = HALF // 16


def tile_list_outcomegatedchain_codednote_kernel(
    tc, xo_words, xo_scales, cq, gs, w_words, w_scales, w2_words, w2_scales,
    wb_words, wb_scales, wc_words, wc_scales, so, sp, bo,
    offs, offs2, offs3, offs4, offs5, offs6, out,
):
    nc = tc.nc
    with ExitStack() as ctx:
        sb = ctx.enter_context(tc.tile_pool(name="sb", bufs=1))
        ps = ctx.enter_context(tc.psum_pool(name="ps", bufs=1))

        def load_list(src, name):
            dst = sb.tile(list(src.shape), U16, name=name)
            nc.sync.dma_start(dst[:], src)
            return dst

        def stage_scales(queue, stage, scales):
            queue.dma_start(out=stage, in_=scales[0].bitcast(I32).rearrange("(q r) n -> r q n", r=4))

        def spread_scales(plane, stage):
            words = plane[:].bitcast(I32)
            for q in range(4):
                nc.vector.tensor_copy(out=words[32 * q : 32 * q + 4, :], in_=stage[:, q, :])

        cq_rows = cq.rearrange("(p t) n -> t p n", t=PACK)
        cq_sb = [sb.tile([P, T], F32, name=f"cq{t}") for t in range(PACK)]


        xo_rows = sb.tile([P, Z], U8)
        nc.vector.memset(xo_rows[:].bitcast(I32), 0)
        l2 = load_list(offs2, "l2")
        ww_stage = sb.tile([4, 4, 2 * R // 4], I32)
        stage_scales(nc.scalar, ww_stage[:, :, 0 : R // 4], w_scales)
        nc.scalar.dma_start(out=cq_sb[0][:], in_=cq_rows[0])
        nc.sync.dma_start(out=xo_rows[:].bitcast(I32)[0:16, :], in_=xo_scales[0].bitcast(I32))
        stage_scales(nc.sync, ww_stage[:, :, R // 4 :], w2_scales)
        l1 = load_list(offs, "l1")
        gs_sb = sb.tile([P, PACK], F32)
        nc.sync.dma_start(out=gs_sb[:], in_=gs.rearrange("(p t) o -> p (t o)", t=PACK))
        w_raw = sb.tile([P, R], U16)
        w2_raw = sb.tile([P, R], U16)
        xo_sb = sb.tile([P, Z], I32)
        for t in range(1, PACK):
            nc.sync.dma_start(out=cq_sb[t][:], in_=cq_rows[t])
        nc.sync.dma_start(out=w_raw[:].bitcast(I32), in_=w_words[0].bitcast(I32))
        nc.sync.dma_start(out=w2_raw[:].bitcast(I32), in_=w2_words[0].bitcast(I32))
        nc.sync.dma_start(out=xo_sb[:], in_=xo_words[0].rearrange("p n t -> p (n t)").bitcast(I32))
        bc_stage = sb.tile([4, 4, 2 * N // 4], I32)
        stage_scales(nc.sync, bc_stage[:, :, 0 : N // 4], wb_scales)
        stage_scales(nc.sync, bc_stage[:, :, N // 4 :], wc_scales)
        wb_sb = sb.tile([P, N], U16, align_bytes=64)
        nc.sync.dma_start(out=wb_sb[:].bitcast(I32), in_=wb_words[0].bitcast(I32))
        l3 = load_list(offs3, "l3")
        wc_sb = sb.tile([P, N], I32, align_bytes=64)
        nc.sync.dma_start(out=wc_sb[:], in_=wc_words[0].rearrange("p n t -> p (n t)").bitcast(I32))
        l4 = load_list(offs4, "l4")
        l6 = load_list(offs6, "l6")
        l5 = load_list(offs5, "l5")
        per_row = []
        with nc.allow_non_contiguous_dma(reason="one value a partition for each block of 128 output features"):
            for name, src in (("so_sb", so), ("sp_sb", sp), ("bo_sb", bo)):
                dst = sb.tile([P, 2], F32, name=name)
                nc.sync.dma_start(out=dst[:], in_=src.rearrange("(h p) o -> p (h o)", p=P))
                per_row.append(dst)
        so_sb, sp_sb, bo_sb = per_row


        warm_in = sb.tile([P, 1], F32)
        warm_out = sb.tile([P, 1], F32)
        nc.vector.memset(warm_in[:], 0.0)
        nc.scalar.activation(out=warm_out[:], in_=warm_in[:], func=ACT.Sigmoid)
        ww_plane = sb.tile([P, 2 * R], U8)
        xo_scale = sb.tile([P, J], U8, align_bytes=64)
        bc_plane = sb.tile([P, 2 * N], U8, align_bytes=64)
        for plane in (xo_scale, ww_plane, bc_plane):
            nc.vector.memset(plane[:].bitcast(I32), 0)
        board = [sb.tile([P, C], F32, name=f"board{h}") for h in range(2)]
        for h in range(2):
            nc.vector.memset(board[h][:], 0.0)

        xo_picked_rows = sb.tile([P, J], U8)
        nc.vector.tensor_copy(out=xo_picked_rows[:], in_=xo_rows[:].indirect(l2[:]))
        nc.vector.tensor_copy(out=xo_scale[:].bitcast(I32)[0:4, :], in_=xo_picked_rows[:].bitcast(I32)[0:4, :])
        for q in range(1, 4):
            nc.scalar.dma_start(
                out=xo_scale[:].bitcast(I32)[32 * q : 32 * q + 4, :],
                in_=xo_picked_rows[:].bitcast(I32)[4 * q : 4 * q + 4, :],
            )

        spread_scales(ww_plane, ww_stage)
        ww_scale = sb.tile([P, 2 * R], U8, align_bytes=64)
        nc.vector.tensor_copy(
            out=ww_scale[:].rearrange("p (w t m) -> p w t m", w=2, t=PACK),
            in_=ww_plane[:].rearrange("p (w m t) -> p w t m", w=2, t=PACK),
        )
        w_sb = sb.tile([P, R], U16, align_bytes=64)
        w2_sb = sb.tile([P, R], U16, align_bytes=64)

        x1_flat = sb.tile([P, PACK * J], BF16)
        x1 = x1_flat[:].rearrange("p (t j) -> p t j", t=PACK)
        for t in range(PACK):
            nc.scalar.activation(
                out=x1[:, t, :], in_=cq_sb[t][:].indirect(l1[:]), func=ACT.Copy, scale=gs_sb[:, t : t + 1]
            )


        def half_cols(u):
            return slice(u * HALF, (u + 1) * HALF)

        def half_list(lst, u):
            return lst[:, u * LIST_COLS : (u + 1) * LIST_COLS]

        def block(t):
            return slice(t * P, (t + 1) * P)

        def quantise(values, name):
            codes = sb.tile([P, HALF], U32, name=name + "_codes", align_bytes=64)
            scale = sb.tile([P, HALF], U8, name=name + "_scale", align_bytes=64)
            nc.vector.quantize_mx(
                out=codes[:].bitcast(FP8X4), scales=scale[:], in_=values[:].rearrange("p j t -> p (j t)")
            )
            return codes, scale

        x1_woven = [sb.tile([P, HALF, PACK], BF16, name=f"x1w{u}", align_bytes=64) for u in range(2)]
        nc.vector.tensor_copy(
            out=x1_woven[0][:, :, 0 : PACK - 1].rearrange("p (c i) t -> p c t i", i=4),
            in_=x1[:, 0 : PACK - 1, half_cols(0)].rearrange("p t (c i) -> p c t i", i=4),
        )
        nc.vector.tensor_copy(
            out=w_sb[:].rearrange("p (t m) -> p t m", t=PACK), in_=w_raw[:].rearrange("p (m t) -> p t m", t=PACK)
        )
        nc.vector.tensor_copy(out=x1_woven[0][:, :, PACK - 1], in_=x1[:, PACK - 1, half_cols(0)])
        nc.scalar.copy(
            out=x1_woven[1][:].rearrange("p (c i) t -> p c t i", i=4),
            in_=x1[:, :, half_cols(1)].rearrange("p t (c i) -> p c t i", i=4),
        )
        nc.scalar.copy(
            out=w2_sb[:].rearrange("p (t m) -> p t m", t=PACK), in_=w2_raw[:].rearrange("p (m t) -> p t m", t=PACK)
        )
        a_sb = []
        b_ps = []
        for u in range(2):
            codes, scale = quantise(x1_woven[u], f"x1q{u}")
            dst = sb.tile([P, 2, HALF, 2], F32, name=f"a_sb{u}")
            for pair in range(2):
                a_ps = ps.tile([P, 2, HALF], F32, name=f"a_ps{u}{pair}", tag=f"bank{u}{pair}")
                for e in range(2):
                    t = 2 * pair + e
                    nc.tensor.matmul_mx(
                        out=a_ps[:, e, :], lhsT=w_sb[:, block(t)].bitcast(FP4X4), lhsT_scale=ww_scale[:, block(t)],
                        rhs=codes[:].bitcast(FP8X4), rhs_scale=scale[:], start=True, stop=True,
                    )
                nc.scalar.copy(out=dst[:, pair, :, :], in_=a_ps[:].rearrange("p e j -> p j e"))
            a_sb.append(dst)

            picked = sb.tile([P, HALF], U32, name=f"xo_pick{u}", align_bytes=64)
            nc.vector.tensor_copy(out=picked[:], in_=xo_sb[:].bitcast(U32).indirect(half_list(l2, u)))
            bank = ps.tile([P, PACK, HALF], F32, name=f"b_ps{u}")
            for t in range(PACK):
                nc.tensor.matmul_mx(
                    out=bank[:, t, :], lhsT=w2_sb[:, block(t)].bitcast(FP4X4),
                    lhsT_scale=ww_scale[:, block(PACK + t)],
                    rhs=picked[:].bitcast(FP8X4), rhs_scale=xo_scale[:, half_cols(u)], start=True, stop=True,
                )
            b_ps.append(bank)

        spread_scales(bc_plane, bc_stage)

        p_ps = [[ps.tile([P, HALF], F32, name=f"p_ps{h}{u}", tag=f"bank{u}{h}") for u in range(2)] for h in range(2)]
        q_ps = ps.tile([P, 2, J], F32, name="q_ps")
        hidq = []
        for u in range(2):
            hid = sb.tile([P, HALF, PACK], BF16, name=f"hid{u}", align_bytes=64)
            nc.vector.tensor_tensor(
                out=hid[:].rearrange("p j (r e) -> p j r e", e=2),
                in0=b_ps[u][:].rearrange("p (r e) j -> p j r e", e=2),
                in1=a_sb[u][:].rearrange("p r j e -> p j r e"),
                op=ALU.max,
            )
            codes, scale = quantise(hid, f"hidq{u}")
            hidq.append((codes, scale))
            for h in range(2):
                nc.tensor.matmul_mx(
                    out=p_ps[h][u][:], lhsT=wb_sb[:, block(h)].bitcast(FP4X4),
                    lhsT_scale=bc_plane[:, block(h)],
                    rhs=codes[:].bitcast(FP8X4), rhs_scale=scale[:], start=True, stop=True,
                )
        for u in range(2):
            p_sb = [sb.tile([P, HALF], F32, name=f"p_sb{h}{u}") for h in range(2)]
            nc.scalar.copy(out=p_sb[0][:], in_=p_ps[0][u][:])
            nc.vector.tensor_copy(out=p_sb[1][:], in_=p_ps[1][u][:])
            nc.scalar.activation(out=board[0][:].indirect(half_list(l3, u)), in_=p_sb[0][:], func=ACT.Copy)
            nc.vector.tensor_copy(out=board[1][:].indirect(half_list(l3, u)), in_=p_sb[1][:])
        for u in range(2):
            codes, scale = hidq[u]
            for h in range(2):
                nc.tensor.matmul_mx(
                    out=q_ps[:, h, half_cols(u)], lhsT=wc_sb[:, block(h)].bitcast(FP8X4),
                    lhsT_scale=bc_plane[:, block(2 + h)],
                    rhs=codes[:].bitcast(FP8X4), rhs_scale=scale[:], start=True, stop=True,
                )

        for h in range(2):
            looked = sb.tile([P, J], F32, name=f"looked{h}")
            nc.vector.tensor_copy(out=looked[:, half_cols(0)], in_=board[h][:].indirect(half_list(l4, 0)))
            nc.scalar.activation(
                out=looked[:, half_cols(1)], in_=board[h][:].indirect(half_list(l4, 1)), func=ACT.Copy
            )
            m0 = sb.tile([P, J], F32, name=f"m0_{h}")
            nc.vector.tensor_tensor(out=m0[:], in0=q_ps[:, h, :], in1=looked[:], op=ALU.max)
            gate = sb.tile([P, O], F32, name=f"gate{h}")
            nc.scalar.activation(
                out=gate[:], in_=m0[:].indirect(l6[:]), func=ACT.Sigmoid,
                scale=sp_sb[:, h : h + 1], bias=bo_sb[:, h : h + 1],
            )
            kept = sb.tile([P, O], F32, name=f"kept{h}")
            nc.scalar.activation(out=kept[:], in_=m0[:].indirect(l5[:]), func=ACT.Copy, scale=so_sb[:, h : h + 1])
            y = sb.tile([P, O], F32, name=f"y{h}")
            nc.vector.tensor_tensor(out=y[:], in0=kept[:], in1=gate[:], op=ALU.mult)
            nc.sync.dma_start(out=out[block(h), :], in_=y[:])
